import numpy as np
import ml_dtypes


def mxq(x, axis, fmt="e4m3"):
    dtype, down = {"e4m3": (ml_dtypes.float8_e4m3fn, 7), "e5m2": (ml_dtypes.float8_e5m2, 14)}[fmt]
    v = np.moveaxis(np.asarray(x, np.float32).astype(ml_dtypes.bfloat16).astype(np.float64), axis, -1)
    blocks = v.reshape(v.shape[:-1] + (-1, 32))
    amax = np.abs(blocks).max(-1, keepdims=True)
    byte = np.maximum(np.where(amax > 0, np.frexp(amax)[1] - 1 + 127, 0) - down, 1)
    scale = np.exp2(byte - 127.0)
    codes = (blocks / scale).astype(np.float32).astype(dtype).astype(np.float64)
    return np.moveaxis((codes * scale).reshape(v.shape), -1, axis)


WIDE = False


def mx_kscale(k):
    if not WIDE:
        return np.ones(k)
    levels = np.array([10, -10, 5, -5, 0])
    if k % 512:
        return np.exp2(np.random.permutation(np.resize(levels, k // 32))).repeat(32)
    a = np.empty((k // 512, 16))
    for p in range(k // 512):
        a[p, :8] = np.random.permutation(np.resize(levels, 8))
        for g in range(8):
            far = levels[np.abs(levels - a[p, g]) >= 10]
            a[p, g + 8] = far[np.random.randint(len(far))]
    return np.exp2(a.ravel()).repeat(32)


def f64(x):
    return np.asarray(x).astype(np.float64)


def striped(idx):
    return np.tile(idx.reshape(-1, 16).T, (8, 1)).astype(np.uint16)


def unstriped(offs):
    return offs[:16].T.reshape(-1).astype(np.int64)


def pack_weight(w):
    k, n = w.shape
    w = f64(np.asarray(w, np.float32).astype(ml_dtypes.bfloat16)).reshape(k // 32, 32, n)
    amax = np.abs(w).max(1)
    byte = np.clip(np.where(amax > 0, np.frexp(amax)[1] - 1 + 127 - 7, 1), 1, 254)
    scaled = (w * np.exp2(127.0 - byte)[:, None, :]).reshape(k, n).astype(np.float32)
    words = np.ascontiguousarray(scaled.reshape(k // 512, 128, 4, n).transpose(0, 1, 3, 2)).astype(ml_dtypes.float8_e4m3fn).view(np.uint8)
    return words, np.ascontiguousarray(byte.astype(np.uint8).reshape(k // 512, 16, n))


def unpack_weight(words, scales):
    g, p, n, _ = words.shape
    vals = np.ascontiguousarray(words).view(ml_dtypes.float8_e4m3fn).astype(np.float64) * np.repeat(np.exp2(scales.astype(np.float64) - 127.0), 8, axis=1)[..., None]
    return vals.transpose(0, 1, 3, 2).reshape(g * 512, n)


E2M1 = np.array([0.0, 0.5, 1.0, 1.5, 2.0, 3.0, 4.0, 6.0, -0.0, -0.5, -1.0, -1.5, -2.0, -3.0, -4.0, -6.0])


def pack_fp4(w):
    k, n = w.shape
    w = f64(np.asarray(w, np.float32).astype(ml_dtypes.bfloat16)).reshape(k // 32, 32, n)
    amax = np.abs(w).max(1)
    mant, ex = np.frexp(amax / 6.0)
    byte = np.clip(np.where(amax > 0, np.where(mant > 0.5, ex, ex - 1) + 127, 1), 1, 254)
    scaled = (w * np.exp2(127.0 - byte)[:, None, :]).reshape(k, n).astype(np.float32)
    c = np.ascontiguousarray(scaled.reshape(k // 512, 128, 4, n).transpose(0, 1, 3, 2)).astype(ml_dtypes.float4_e2m1fn).view(np.uint8) & 0xF
    words = (c[..., 0::2] | (c[..., 1::2] << 4)).reshape(k // 512, 128, 2 * n)
    return np.ascontiguousarray(words), np.ascontiguousarray(byte.astype(np.uint8).reshape(k // 512, 16, n))


def unpack_fp4(words, scales):
    g, _, n = scales.shape
    words = np.ascontiguousarray(words).reshape(g, 128, n, 2)
    nib = np.empty((g, 128, n, 4), np.uint8)
    nib[..., 0::2] = words & 0xF
    nib[..., 1::2] = words >> 4
    vals = E2M1[nib] * np.repeat(np.exp2(scales.astype(np.float64) - 127.0), 8, axis=1)[..., None]
    return vals.transpose(0, 1, 3, 2).reshape(g * 512, n)


def planes(y):
    n, m = y.shape
    v = y.astype(np.float32).astype(ml_dtypes.bfloat16).astype(np.float64).reshape(n // 32, 32, m)
    top = np.abs(v).max(1)
    byte = np.clip(np.where(top > 0, np.frexp(top)[1] - 1 + 127 - 7, 1), 1, 254)
    codes = (v * np.exp2(127.0 - byte)[:, None, :]).reshape(n, m).astype(np.float32).astype(ml_dtypes.float8_e4m3fn).view(np.uint8)
    words = codes.reshape(n // 512, 128, 4, m).transpose(0, 1, 3, 2)
    return np.ascontiguousarray(words), np.ascontiguousarray(byte.astype(np.uint8).reshape(n // 512, 16, m))


K, T, S, N = 512, 1024, 512, 512


def setup_inputs():
    n = np.random.standard_normal
    s = mx_kscale(K)[:, None]
    packed_xT = pack_weight(n((K, T)) * s)
    packed_w1 = pack_fp4(n((K, N)) / np.sqrt(2 * K) / s)
    packed_w2 = pack_fp4(n((K, N)) / np.sqrt(2 * K) / s)
    packed_w3 = pack_fp4(n((K, N)) / np.sqrt(2 * K) / s)
    packed_w4 = pack_fp4(n((K, N)) / np.sqrt(2 * K) / s)
    return {
        "x_words": packed_xT[0],
        "x_scales": packed_xT[1],
        "eT": (n((K, S)) * s).astype(np.float32),
        "w1_words": packed_w1[0],
        "w1_scales": packed_w1[1],
        "w2_words": packed_w2[0],
        "w2_scales": packed_w2[1],
        "w3_words": packed_w3[0],
        "w3_scales": packed_w3[1],
        "w4_words": packed_w4[0],
        "w4_scales": packed_w4[1],
        "dec": (n((N, S))).astype(np.float32),
        "offs": striped(np.random.permutation(T)[:S]),
    }


def reference(x_words, x_scales, eT, w1_words, w1_scales, w2_words, w2_scales, w3_words, w3_scales, w4_words, w4_scales, dec, offs):
    eTq = mxq(f64(eT), 0, "e4m3")
    xq = unpack_weight(x_words, x_scales)[:, unstriped(offs)]
    g = unpack_fp4(w1_words, w1_scales).T @ eTq + unpack_fp4(w2_words, w2_scales).T @ xq
    h = unpack_fp4(w3_words, w3_scales).T @ eTq + unpack_fp4(w4_words, w4_scales).T @ xq
    out_0 = f64(dec) * g + h + f64(dec)
    return (out_0,) + planes(out_0)

@@ -1,0 +1,185 @@
+from contextlib import ExitStack
+
+import concourse.mybir as mybir
+
+K, T, S, N = 512, 1024, 512, 512
+FLOPS = 4 * 2 * K * N * S
+
+F32 = mybir.dt.float32
+BF16 = mybir.dt.bfloat16
+I32 = mybir.dt.int32
+U32 = mybir.dt.uint32
+U16 = mybir.dt.uint16
+U8 = mybir.dt.uint8
+FP8X4 = mybir.dt.float8_e4m3fn_x4
+FP4X4 = mybir.dt.float4_e2m1fn_x4
+ADD = mybir.AluOpType.add
+MULT = mybir.AluOpType.mult
+
+P = 128
+PACK = 4
+BANK = 512
+HALF = S // 2
+PIECES = ((0, 256), (256, 128), (384, 128))
+
+
+def interleave(copy, dst, src):
+    copy(
+        out=dst.rearrange("p (c i) t -> p c t i", i=4),
+        in_=src.rearrange("p t (c i) -> p c t i", i=4),
+    )
+
+
+def tile_picked_zcft_add_po_kernel(
+    tc, x_words, x_scales, eT, w1_words, w1_scales, w2_words, w2_scales, w3_words, w3_scales,
+    w4_words, w4_scales, dec, offs, out_0, out_1, out_2,
+):
+    nc = tc.nc
+    w_words = (w1_words, w2_words, w3_words, w4_words)
+    w_scales = (w1_scales, w2_scales, w3_scales, w4_scales)
+    halves = [slice(0, HALF), slice(HALF, S)]
+    e_rows = eT.rearrange("(p t) j -> p t j", t=PACK)
+    dec_rows = dec.rearrange("(p t) j -> p t j", t=PACK)
+    out_rows = out_0.rearrange("(p t) j -> p t j", t=PACK)
+    out_words = out_1[0].rearrange("p j t -> p (j t)").bitcast(I32)
+
+    with ExitStack() as ctx:
+        keep = ctx.enter_context(tc.tile_pool(name="keep", bufs=1))
+        psum = ctx.enter_context(tc.psum_pool(name="psum", bufs=1))
+
+        def sbuf(name, shape, dtype, tag=None):
+            return keep.tile(shape, dtype, name=name, tag=tag or name, align_bytes=64)
+
+        def pair(name, shape, dtype):
+            return [sbuf("%s%d" % (name, c), shape, dtype) for c in range(2)]
+
+        offsets = keep.tile([P, S // 16], U16, name="offsets")
+        ws_raw = sbuf("ws_raw", [P, N], U8)
+        ws_dealt = sbuf("ws_dealt", [P, N], U8)
+        w_plane = sbuf("w_plane", [P, 4 * N], U8)
+        ww_dealt = [sbuf("ww_dealt%d" % w, [P, 2 * N], U8) for w in range(4)]
+        xw_table = sbuf("xw_table", [P, T], U32)
+        out_plane = sbuf("out_plane", [P, S], U8)
+        e_codes = pair("e_codes", [P, HALF], U32)
+        e_plane = pair("e_plane", [P, HALF], U8)
+        x_codes = pair("x_codes", [P, HALF], U32)
+        x_plane = pair("x_plane", [P, HALF], U8)
+
+        nc.gpsimd.memset(ws_raw[64:P, :].bitcast(I32), 0)
+        nc.gpsimd.memset(w_plane[:].bitcast(I32), 0)
+
+        def load_words(w, tag):
+            raw = sbuf("ww_raw%d" % w, [P, 2 * N], U8, tag)
+            nc.sync.dma_start(out=raw[:].bitcast(I32), in_=w_words[w][0].bitcast(I32))
+            return raw
+
+        def deal_words(w, raw):
+            nc.scalar.copy(
+                out=ww_dealt[w][:].bitcast(U16).rearrange("p (t b i) -> p b t i", t=PACK, i=8),
+                in_=raw[:].bitcast(U16).rearrange("p (b i t) -> p b t i", t=PACK, i=8),
+            )
+
+        def load_rows(name, rows, c, tag):
+            raw = sbuf("%s%d" % (name, c), [P, PACK, HALF], F32, tag)
+            nc.sync.dma_start(out=raw[:], in_=rows[:, :, halves[c]])
+            return raw
+
+        def quantize_e(c, copy, raw):
+            grouped = sbuf("e_bf%d" % c, [P, HALF, PACK], BF16)
+            interleave(copy, grouped[:], raw[:])
+            nc.vector.quantize_mx(
+                out=e_codes[c][:].bitcast(FP8X4), scales=e_plane[c][:], in_=grouped[:].rearrange("p j t -> p (j t)")
+            )
+
+        def entries(c):
+            return offsets[:, c * HALF // 16 : (c + 1) * HALF // 16]
+
+        for w in range(4):
+            nc.sync.dma_start(out=ws_raw[w:64:4, :].bitcast(I32), in_=w_scales[w][0].bitcast(I32))
+        w1_raw = load_words(0, "ww_a")
+        w3_raw = load_words(2, "ww_b")
+        e_raw0 = load_rows("e_raw", e_rows, 0, "rows_a")
+        nc.sync.dma_start(out=xw_table[:].bitcast(I32), in_=x_words[0].rearrange("p n t -> p (n t)").bitcast(I32))
+        nc.sync.dma_start(offsets[:], offs)
+
+        nc.vector.tensor_copy(
+            out=ws_dealt[:].rearrange("p (t b i) -> p b t i", t=PACK, i=16),
+            in_=ws_raw[:].rearrange("p (b i t) -> p b t i", t=PACK, i=16),
+        )
+        for q in range(4):
+            nc.scalar.dma_start(
+                out=w_plane[32 * q : 32 * q + 4, :].bitcast(I32).rearrange("r (w n) -> r w n", w=4),
+                in_=ws_dealt[16 * q : 16 * q + 16, :].bitcast(I32),
+            )
+        deal_words(0, w1_raw)
+        deal_words(2, w3_raw)
+        w2_raw = load_words(1, "ww_a")
+        w4_raw = load_words(3, "ww_b")
+
+        xs_table = sbuf("xs_table", [P, T], U8, "ws_raw")
+        nc.gpsimd.memset(xs_table[:].bitcast(I32), 0)
+        for q in range(4):
+            nc.sync.dma_start(
+                out=xs_table[32 * q : 32 * q + 4, :].bitcast(I32), in_=x_scales[0, 4 * q : 4 * q + 4, :].bitcast(I32)
+            )
+        quantize_e(0, nc.vector.tensor_copy, e_raw0)
+        dec_sb = [load_rows("dec_sb", dec_rows, 0, "rows_a")]
+        e_raw1 = load_rows("e_raw", e_rows, 1, "ws_dealt")
+        dec_sb.append(load_rows("dec_sb", dec_rows, 1, "e_bf0"))
+        deal_words(1, w2_raw)
+        deal_words(3, w4_raw)
+        for c in range(2):
+            nc.vector.tensor_copy(x_codes[c][:], xw_table[:].indirect(entries(c)))
+        for c in range(2):
+            nc.vector.tensor_copy(x_plane[c][:], xs_table[:].indirect(entries(c)))
+        quantize_e(1, nc.scalar.copy, e_raw1)
+
+        def product(c, part, bank, ts, w_e, w_x):
+            for w, codes, plane in ((w_e, e_codes, e_plane), (w_x, x_codes, x_plane)):
+                for i, t in enumerate(ts):
+                    nc.tensor.matmul_mx(
+                        out=bank[:, i, :],
+                        lhsT=ww_dealt[w][:, 2 * P * t : 2 * P * (t + 1)].bitcast(FP4X4),
+                        lhsT_scale=w_plane[:, N * w + P * t : N * w + P * (t + 1)],
+                        rhs=codes[c][:, part].bitcast(FP8X4),
+                        rhs_scale=plane[c][:, part],
+                        start=(w == w_e and t == ts[0]),
+                        stop=(w == w_x and t == ts[-1]),
+                    )
+
+        for n, (first, width) in enumerate(PIECES):
+            c = first // HALF
+            cols = slice(first, first + width)
+            part = slice(first - c * HALF, first - c * HALF + width)
+            per_bank = BANK // width
+            groups = [range(t0, t0 + per_bank) for t0 in range(0, PACK, per_bank)]
+            g_banks = [psum.tile([P, per_bank, width], F32, name="g%d_%d" % (n, b)) for b in range(len(groups))]
+            h_banks = [psum.tile([P, per_bank, width], F32, name="h%d_%d" % (n, b)) for b in range(len(groups))]
+            res = sbuf("res%d" % n, [P, PACK, width], F32)
+            res_bf = sbuf("res_bf%d" % n, [P, width, PACK], BF16)
+            res_codes = sbuf("res_codes%d" % n, [P, width], U32)
+            for ts, bank in zip(groups, g_banks):
+                product(c, part, bank, ts, 0, 1)
+            for ts, bank in zip(groups, h_banks):
+                product(c, part, bank, ts, 2, 3)
+            for ts, bank in zip(groups, g_banks):
+                rows = slice(ts.start, ts.stop)
+                nc.vector.scalar_tensor_tensor(
+                    out=res[:, rows, :], in0=bank[:], scalar=1.0, in1=dec_sb[c][:, rows, part], op0=ADD, op1=MULT
+                )
+            for ts, bank in zip(groups, h_banks):
+                rows = slice(ts.start, ts.stop)
+                nc.vector.tensor_tensor(out=res[:, rows, :], in0=bank[:], in1=res[:, rows, :], op=ADD)
+            nc.sync.dma_start(out=out_rows[:, :, cols], in_=res[:])
+            last = n == len(PIECES) - 1
+            interleave(nc.vector.tensor_copy if last else nc.scalar.copy, res_bf[:], res[:])
+            nc.vector.quantize_mx(
+                out=res_codes[:].bitcast(FP8X4), scales=out_plane[:, cols], in_=res_bf[:].rearrange("p j t -> p (j t)")
+            )
+            nc.sync.dma_start(out=out_words[:, cols], in_=res_codes[:].bitcast(I32))
+
+        for q in range(4):
+            queue = nc.scalar if q % 2 else nc.sync
+            queue.dma_start(
+                out=out_2[0, 4 * q : 4 * q + 4, :].bitcast(I32), in_=out_plane[32 * q : 32 * q + 4, :].bitcast(I32)
+            )

@@ -20,7 +20,8 @@ P = 128
 PACK = 4
 BANK = 512
 HALF = S // 2
-PIECES = ((0, 256), (256, 128), (384, 128))
+VECTOR_SHARE = 168
+PIECES = ((0, 256), (256, 256))
 
 
 def interleave(copy, dst, src):
@@ -65,18 +66,19 @@ def tile_picked_zcft_add_po_kernel(
         x_codes = pair("x_codes", [P, HALF], U32)
         x_plane = pair("x_plane", [P, HALF], U8)
 
-        nc.gpsimd.memset(ws_raw[64:P, :].bitcast(I32), 0)
-        nc.gpsimd.memset(w_plane[:].bitcast(I32), 0)
+        xs_table = sbuf("xs_table", [P, T], U8)
+        nc.gpsimd.memset(xs_table[:].bitcast(I32), 0)
+        nc.vector.memset(ws_raw[64:P, :].bitcast(I32), 0)
+        nc.vector.memset(w_plane[:].bitcast(I32), 0)
 
-        def load_words(w, tag):
-            raw = sbuf("ww_raw%d" % w, [P, 2 * N], U8, tag)
-            nc.sync.dma_start(out=raw[:].bitcast(I32), in_=w_words[w][0].bitcast(I32))
+        def load_words(w, queue, raw):
+            queue.dma_start(out=raw.bitcast(I32), in_=w_words[w][0].bitcast(I32))
             return raw
 
         def deal_words(w, raw):
             nc.scalar.copy(
                 out=ww_dealt[w][:].bitcast(U16).rearrange("p (t b i) -> p b t i", t=PACK, i=8),
-                in_=raw[:].bitcast(U16).rearrange("p (b i t) -> p b t i", t=PACK, i=8),
+                in_=raw.bitcast(U16).rearrange("p (b i t) -> p b t i", t=PACK, i=8),
             )
 
         def load_rows(name, rows, c, tag):
@@ -84,8 +86,8 @@ def tile_picked_zcft_add_po_kernel(
             nc.sync.dma_start(out=raw[:], in_=rows[:, :, halves[c]])
             return raw
 
-        def quantize_e(c, copy, raw):
-            grouped = sbuf("e_bf%d" % c, [P, HALF, PACK], BF16)
+        def quantize_e(c, copy, raw, tag):
+            grouped = sbuf("e_bf%d" % c, [P, HALF, PACK], BF16, tag)
             interleave(copy, grouped[:], raw[:])
             nc.vector.quantize_mx(
                 out=e_codes[c][:].bitcast(FP8X4), scales=e_plane[c][:], in_=grouped[:].rearrange("p j t -> p (j t)")
@@ -96,11 +98,16 @@ def tile_picked_zcft_add_po_kernel(
 
         for w in range(4):
             nc.sync.dma_start(out=ws_raw[w:64:4, :].bitcast(I32), in_=w_scales[w][0].bitcast(I32))
-        w1_raw = load_words(0, "ww_a")
-        w3_raw = load_words(2, "ww_b")
-        e_raw0 = load_rows("e_raw", e_rows, 0, "rows_a")
-        nc.sync.dma_start(out=xw_table[:].bitcast(I32), in_=x_words[0].rearrange("p n t -> p (n t)").bitcast(I32))
         nc.sync.dma_start(offsets[:], offs)
+        w1_raw = load_words(0, nc.sync, sbuf("w1_raw", [P, 2 * N], U8)[:])
+        e_raw0 = load_rows("e_raw", e_rows, 0, "e_raw0")
+        nc.sync.dma_start(out=xw_table[:].bitcast(I32), in_=x_words[0].rearrange("p n t -> p (n t)").bitcast(I32))
+        w2_raw = load_words(1, nc.sync, sbuf("w2_raw", [P, 2 * N], U8)[:])
+        dec_sb = [load_rows("dec_sb", dec_rows, 0, "dec_sb0")]
+        for q in range(4):
+            nc.gpsimd.dma_start(
+                out=xs_table[32 * q : 32 * q + 4, :].bitcast(I32), in_=x_scales[0, 4 * q : 4 * q + 4, :].bitcast(I32)
+            )
 
         nc.vector.tensor_copy(
             out=ws_dealt[:].rearrange("p (t b i) -> p b t i", t=PACK, i=16),
@@ -111,28 +118,21 @@ def tile_picked_zcft_add_po_kernel(
                 out=w_plane[32 * q : 32 * q + 4, :].bitcast(I32).rearrange("r (w n) -> r w n", w=4),
                 in_=ws_dealt[16 * q : 16 * q + 16, :].bitcast(I32),
             )
+        shift_raw = sbuf("shift_raw", [P, 4 * N], U8, "ws_raw")
+        w3_raw = load_words(2, nc.gpsimd, shift_raw[:, : 2 * N])
+        w4_raw = load_words(3, nc.gpsimd, shift_raw[:, 2 * N :])
         deal_words(0, w1_raw)
-        deal_words(2, w3_raw)
-        w2_raw = load_words(1, "ww_a")
-        w4_raw = load_words(3, "ww_b")
-
-        xs_table = sbuf("xs_table", [P, T], U8, "ws_raw")
-        nc.gpsimd.memset(xs_table[:].bitcast(I32), 0)
-        for q in range(4):
-            nc.sync.dma_start(
-                out=xs_table[32 * q : 32 * q + 4, :].bitcast(I32), in_=x_scales[0, 4 * q : 4 * q + 4, :].bitcast(I32)
-            )
-        quantize_e(0, nc.vector.tensor_copy, e_raw0)
-        dec_sb = [load_rows("dec_sb", dec_rows, 0, "rows_a")]
-        e_raw1 = load_rows("e_raw", e_rows, 1, "ws_dealt")
-        dec_sb.append(load_rows("dec_sb", dec_rows, 1, "e_bf0"))
+        e_raw1 = load_rows("e_raw", e_rows, 1, "w1_raw")
+        quantize_e(0, nc.vector.tensor_copy, e_raw0, "e_bf0")
+        dec_sb.append(load_rows("dec_sb", dec_rows, 1, "e_raw0"))
         deal_words(1, w2_raw)
-        deal_words(3, w4_raw)
         for c in range(2):
             nc.vector.tensor_copy(x_codes[c][:], xw_table[:].indirect(entries(c)))
         for c in range(2):
             nc.vector.tensor_copy(x_plane[c][:], xs_table[:].indirect(entries(c)))
-        quantize_e(1, nc.scalar.copy, e_raw1)
+        deal_words(2, w3_raw)
+        deal_words(3, w4_raw)
+        quantize_e(1, nc.scalar.copy, e_raw1, "ws_raw")
 
         def product(c, part, bank, ts, w_e, w_x):
             for w, codes, plane in ((w_e, e_codes, e_plane), (w_x, x_codes, x_plane)):
@@ -171,8 +171,10 @@ def tile_picked_zcft_add_po_kernel(
                 rows = slice(ts.start, ts.stop)
                 nc.vector.tensor_tensor(out=res[:, rows, :], in0=bank[:], in1=res[:, rows, :], op=ADD)
             nc.sync.dma_start(out=out_rows[:, :, cols], in_=res[:])
-            last = n == len(PIECES) - 1
-            interleave(nc.vector.tensor_copy if last else nc.scalar.copy, res_bf[:], res[:])
+            split = VECTOR_SHARE if n == len(PIECES) - 1 else 0
+            if split:
+                interleave(nc.vector.tensor_copy, res_bf[:, :split, :], res[:, :, :split])
+            interleave(nc.scalar.copy, res_bf[:, split:, :], res[:, :, split:])
             nc.vector.quantize_mx(
                 out=res_codes[:].bitcast(FP8X4), scales=out_plane[:, cols], in_=res_bf[:].rearrange("p j t -> p (j t)")
             )

@@ -19,9 +19,9 @@ MULT = mybir.AluOpType.mult
 P = 128
 PACK = 4
 BANK = 512
-HALF = S // 2
-VECTOR_SHARE = 168
-PIECES = ((0, 256), (256, 256))
+PIECES = ((0, 256), (256, 128), (384, 128))
+EARLY = 256
+W1, W2, W3, W4 = range(4)
 
 
 def interleave(copy, dst, src):
@@ -38,7 +38,6 @@ def tile_picked_zcft_add_po_kernel(
     nc = tc.nc
     w_words = (w1_words, w2_words, w3_words, w4_words)
     w_scales = (w1_scales, w2_scales, w3_scales, w4_scales)
-    halves = [slice(0, HALF), slice(HALF, S)]
     e_rows = eT.rearrange("(p t) j -> p t j", t=PACK)
     dec_rows = dec.rearrange("(p t) j -> p t j", t=PACK)
     out_rows = out_0.rearrange("(p t) j -> p t j", t=PACK)
@@ -51,25 +50,19 @@ def tile_picked_zcft_add_po_kernel(
         def sbuf(name, shape, dtype, tag=None):
             return keep.tile(shape, dtype, name=name, tag=tag or name, align_bytes=64)
 
-        def pair(name, shape, dtype):
-            return [sbuf("%s%d" % (name, c), shape, dtype) for c in range(2)]
-
         offsets = keep.tile([P, S // 16], U16, name="offsets")
-        ws_raw = sbuf("ws_raw", [P, N], U8)
-        ws_dealt = sbuf("ws_dealt", [P, N], U8)
+        ws_raw = sbuf("ws_raw", [P, 4 * N], U8)
         w_plane = sbuf("w_plane", [P, 4 * N], U8)
         ww_dealt = [sbuf("ww_dealt%d" % w, [P, 2 * N], U8) for w in range(4)]
         xw_table = sbuf("xw_table", [P, T], U32)
-        out_plane = sbuf("out_plane", [P, S], U8)
-        e_codes = pair("e_codes", [P, HALF], U32)
-        e_plane = pair("e_plane", [P, HALF], U8)
-        x_codes = pair("x_codes", [P, HALF], U32)
-        x_plane = pair("x_plane", [P, HALF], U8)
-
         xs_table = sbuf("xs_table", [P, T], U8)
+        x_codes = sbuf("x_codes", [P, S], U32)
+        x_plane = sbuf("x_plane", [P, S], U8)
+        out_plane = sbuf("out_plane", [P, S], U8)
+
         nc.gpsimd.memset(xs_table[:].bitcast(I32), 0)
+        nc.vector.memset(ws_raw[32:64, :].bitcast(I32), 0)
         nc.vector.memset(ws_raw[64:P, :].bitcast(I32), 0)
-        nc.vector.memset(w_plane[:].bitcast(I32), 0)
 
         def load_words(w, queue, raw):
             queue.dma_start(out=raw.bitcast(I32), in_=w_words[w][0].bitcast(I32))
@@ -81,76 +74,87 @@ def tile_picked_zcft_add_po_kernel(
                 in_=raw.bitcast(U16).rearrange("p (b i t) -> p b t i", t=PACK, i=8),
             )
 
-        def load_rows(name, rows, c, tag):
-            raw = sbuf("%s%d" % (name, c), [P, PACK, HALF], F32, tag)
-            nc.sync.dma_start(out=raw[:], in_=rows[:, :, halves[c]])
-            return raw
-
-        def quantize_e(c, copy, raw, tag):
-            grouped = sbuf("e_bf%d" % c, [P, HALF, PACK], BF16, tag)
-            interleave(copy, grouped[:], raw[:])
-            nc.vector.quantize_mx(
-                out=e_codes[c][:].bitcast(FP8X4), scales=e_plane[c][:], in_=grouped[:].rearrange("p j t -> p (j t)")
-            )
-
-        def entries(c):
-            return offsets[:, c * HALF // 16 : (c + 1) * HALF // 16]
-
-        for w in range(4):
-            nc.sync.dma_start(out=ws_raw[w:64:4, :].bitcast(I32), in_=w_scales[w][0].bitcast(I32))
-        nc.sync.dma_start(offsets[:], offs)
-        w1_raw = load_words(0, nc.sync, sbuf("w1_raw", [P, 2 * N], U8)[:])
-        e_raw0 = load_rows("e_raw", e_rows, 0, "e_raw0")
-        nc.sync.dma_start(out=xw_table[:].bitcast(I32), in_=x_words[0].rearrange("p n t -> p (n t)").bitcast(I32))
-        w2_raw = load_words(1, nc.sync, sbuf("w2_raw", [P, 2 * N], U8)[:])
-        dec_sb = [load_rows("dec_sb", dec_rows, 0, "dec_sb0")]
-        for q in range(4):
-            nc.gpsimd.dma_start(
+        def load_x_scales(q):
+            nc.sync.dma_start(
                 out=xs_table[32 * q : 32 * q + 4, :].bitcast(I32), in_=x_scales[0, 4 * q : 4 * q + 4, :].bitcast(I32)
             )
 
-        nc.vector.tensor_copy(
-            out=ws_dealt[:].rearrange("p (t b i) -> p b t i", t=PACK, i=16),
-            in_=ws_raw[:].rearrange("p (b i t) -> p b t i", t=PACK, i=16),
-        )
-        for q in range(4):
-            nc.scalar.dma_start(
-                out=w_plane[32 * q : 32 * q + 4, :].bitcast(I32).rearrange("r (w n) -> r w n", w=4),
-                in_=ws_dealt[16 * q : 16 * q + 16, :].bitcast(I32),
-            )
-        shift_raw = sbuf("shift_raw", [P, 4 * N], U8, "ws_raw")
-        w3_raw = load_words(2, nc.gpsimd, shift_raw[:, : 2 * N])
-        w4_raw = load_words(3, nc.gpsimd, shift_raw[:, 2 * N :])
-        deal_words(0, w1_raw)
-        e_raw1 = load_rows("e_raw", e_rows, 1, "w1_raw")
-        quantize_e(0, nc.vector.tensor_copy, e_raw0, "e_bf0")
-        dec_sb.append(load_rows("dec_sb", dec_rows, 1, "e_raw0"))
-        deal_words(1, w2_raw)
-        for c in range(2):
-            nc.vector.tensor_copy(x_codes[c][:], xw_table[:].indirect(entries(c)))
-        for c in range(2):
-            nc.vector.tensor_copy(x_plane[c][:], xs_table[:].indirect(entries(c)))
-        deal_words(2, w3_raw)
-        deal_words(3, w4_raw)
-        quantize_e(1, nc.scalar.copy, e_raw1, "ws_raw")
+        def load_rows(rows, cols, raw):
+            nc.sync.dma_start(out=raw, in_=rows[:, :, cols])
+            return raw
 
-        def product(c, part, bank, ts, w_e, w_x):
-            for w, codes, plane in ((w_e, e_codes, e_plane), (w_x, x_codes, x_plane)):
+        def quantize_e(n, copy, raw):
+            width = PIECES[n][1]
+            grouped = sbuf("e_bf%d" % n, [P, width, PACK], BF16)
+            codes = sbuf("e_codes%d" % n, [P, width], U32)
+            plane = sbuf("e_plane%d" % n, [P, width], U8)
+            interleave(copy, grouped[:], raw)
+            nc.vector.quantize_mx(out=codes[:].bitcast(FP8X4), scales=plane[:], in_=grouped[:].rearrange("p j t -> p (j t)"))
+            return codes[:], plane[:]
+
+        early, late = slice(0, EARLY), slice(EARLY, S)
+        for w in range(4):
+            nc.sync.dma_start(
+                out=ws_raw[0:32, N * w : N * (w + 1)].bitcast(I32), in_=w_scales[w][0].bitcast(I32).partition_broadcast(2)
+            )
+        nc.sync.dma_start(offsets[:], offs)
+        ww_raw = {W2: load_words(W2, nc.gpsimd, sbuf("w2_raw", [P, 2 * N], U8)[:])}
+        load_x_scales(0)
+        load_x_scales(1)
+        nc.sync.dma_start(out=xw_table[:].bitcast(I32), in_=x_words[0].rearrange("p n t -> p (n t)").bitcast(I32))
+        load_x_scales(2)
+        load_x_scales(3)
+        e_raw = [load_rows(e_rows, early, sbuf("e_early", [P, PACK, EARLY], F32)[:])]
+        ww_raw[W1] = load_words(W1, nc.sync, sbuf("w1_raw", [P, 2 * N], U8)[:])
+        nc.vector.tensor_copy(
+            out=w_plane[:].rearrange("p (w t b i) -> p w b t i", w=4, t=PACK, i=16),
+            in_=ws_raw[:].rearrange("p (w b i t) -> p w b t i", w=4, t=PACK, i=16),
+        )
+        for q in range(1, 4):
+            nc.sync.dma_start(
+                out=w_plane[32 * q : 32 * q + 4, :].bitcast(I32), in_=w_plane[4 * q : 4 * q + 4, :].bitcast(I32)
+            )
+        dec_sb = [load_rows(dec_rows, early, sbuf("dec_early", [P, PACK, EARLY], F32, "ws_raw")[:])]
+        nc.vector.tensor_copy(x_codes[:], xw_table[:].indirect(offsets[:]))
+        shift_raw = sbuf("shift_raw", [P, 4 * N], U8, "xw_table")
+        ww_raw[W4] = load_words(W4, nc.sync, shift_raw[:, : 2 * N])
+        ww_raw[W3] = load_words(W3, nc.sync, shift_raw[:, 2 * N :])
+        nc.vector.tensor_copy(x_plane[:], xs_table[:].indirect(offsets[:]))
+        late_rows = sbuf("late_rows", [P, 2, PACK, S - EARLY], F32, "xs_table")
+        e_raw.append(load_rows(e_rows, late, late_rows[:, 0]))
+        dec_sb.append(load_rows(dec_rows, late, late_rows[:, 1]))
+
+        def part(tiles, n):
+            first, width = PIECES[n]
+            if first < EARLY:
+                return tiles[0][:, :, first : first + width]
+            return tiles[1][:, :, first - EARLY : first - EARLY + width]
+
+        e_mx = [quantize_e(0, nc.vector.tensor_copy, part(e_raw, 0))]
+        for w in (W2, W1, W4, W3):
+            deal_words(w, ww_raw[w])
+        e_mx.extend([quantize_e(n, nc.scalar.copy, part(e_raw, n)) for n in (1, 2)])
+
+        def product(n, bank, ts, w_first, w_last):
+            first, width = PIECES[n]
+            for w in (w_first, w_last):
+                if w in (W1, W3):
+                    codes, plane = e_mx[n]
+                else:
+                    codes, plane = x_codes[:, first : first + width], x_plane[:, first : first + width]
                 for i, t in enumerate(ts):
                     nc.tensor.matmul_mx(
                         out=bank[:, i, :],
                         lhsT=ww_dealt[w][:, 2 * P * t : 2 * P * (t + 1)].bitcast(FP4X4),
                         lhsT_scale=w_plane[:, N * w + P * t : N * w + P * (t + 1)],
-                        rhs=codes[c][:, part].bitcast(FP8X4),
-                        rhs_scale=plane[c][:, part],
-                        start=(w == w_e and t == ts[0]),
-                        stop=(w == w_x and t == ts[-1]),
+                        rhs=codes.bitcast(FP8X4),
+                        rhs_scale=plane,
+                        start=(w == w_first and t == ts[0]),
+                        stop=(w == w_last and t == ts[-1]),
                     )
 
         for n, (first, width) in enumerate(PIECES):
-            c = first // HALF
             cols = slice(first, first + width)
-            part = slice(first - c * HALF, first - c * HALF + width)
             per_bank = BANK // width
             groups = [range(t0, t0 + per_bank) for t0 in range(0, PACK, per_bank)]
             g_banks = [psum.tile([P, per_bank, width], F32, name="g%d_%d" % (n, b)) for b in range(len(groups))]
@@ -158,23 +162,22 @@ def tile_picked_zcft_add_po_kernel(
             res = sbuf("res%d" % n, [P, PACK, width], F32)
             res_bf = sbuf("res_bf%d" % n, [P, width, PACK], BF16)
             res_codes = sbuf("res_codes%d" % n, [P, width], U32)
+            dec_part = part(dec_sb, n)
             for ts, bank in zip(groups, g_banks):
-                product(c, part, bank, ts, 0, 1)
+                product(n, bank, ts, W2, W1)
             for ts, bank in zip(groups, h_banks):
-                product(c, part, bank, ts, 2, 3)
+                product(n, bank, ts, W4, W3)
             for ts, bank in zip(groups, g_banks):
                 rows = slice(ts.start, ts.stop)
                 nc.vector.scalar_tensor_tensor(
-                    out=res[:, rows, :], in0=bank[:], scalar=1.0, in1=dec_sb[c][:, rows, part], op0=ADD, op1=MULT
+                    out=res[:, rows, :], in0=bank[:], scalar=1.0, in1=dec_part[:, rows, :], op0=ADD, op1=MULT
                 )
             for ts, bank in zip(groups, h_banks):
                 rows = slice(ts.start, ts.stop)
                 nc.vector.tensor_tensor(out=res[:, rows, :], in0=bank[:], in1=res[:, rows, :], op=ADD)
             nc.sync.dma_start(out=out_rows[:, :, cols], in_=res[:])
-            split = VECTOR_SHARE if n == len(PIECES) - 1 else 0
-            if split:
-                interleave(nc.vector.tensor_copy, res_bf[:, :split, :], res[:, :, :split])
-            interleave(nc.scalar.copy, res_bf[:, split:, :], res[:, :, split:])
+            last = n == len(PIECES) - 1
+            interleave(nc.vector.tensor_copy if last else nc.scalar.copy, res_bf[:], res[:])
             nc.vector.quantize_mx(
                 out=res_codes[:].bitcast(FP8X4), scales=out_plane[:, cols], in_=res_bf[:].rearrange("p j t -> p (j t)")
             )

@@ -20,7 +20,7 @@ P = 128
 PACK = 4
 BANK = 512
 PIECES = ((0, 256), (256, 128), (384, 128))
-EARLY = 256
+EARLY = 384
 W1, W2, W3, W4 = range(4)
 
 
@@ -104,8 +104,8 @@ def tile_picked_zcft_add_po_kernel(
         nc.sync.dma_start(out=xw_table[:].bitcast(I32), in_=x_words[0].rearrange("p n t -> p (n t)").bitcast(I32))
         load_x_scales(2)
         load_x_scales(3)
-        e_raw = [load_rows(e_rows, early, sbuf("e_early", [P, PACK, EARLY], F32)[:])]
         ww_raw[W1] = load_words(W1, nc.sync, sbuf("w1_raw", [P, 2 * N], U8)[:])
+        e_raw = [load_rows(e_rows, early, sbuf("e_early", [P, PACK, EARLY], F32)[:])]
         nc.vector.tensor_copy(
             out=w_plane[:].rearrange("p (w t b i) -> p w b t i", w=4, t=PACK, i=16),
             in_=ws_raw[:].rearrange("p (w b i t) -> p w b t i", w=4, t=PACK, i=16),
@@ -131,9 +131,10 @@ def tile_picked_zcft_add_po_kernel(
             return tiles[1][:, :, first - EARLY : first - EARLY + width]
 
         e_mx = [quantize_e(0, nc.vector.tensor_copy, part(e_raw, 0))]
-        for w in (W2, W1, W4, W3):
-            deal_words(w, ww_raw[w])
-        e_mx.extend([quantize_e(n, nc.scalar.copy, part(e_raw, n)) for n in (1, 2)])
+        for n, pair in ((1, (W2, W1)), (2, (W4, W3))):
+            for w in pair:
+                deal_words(w, ww_raw[w])
+            e_mx.append(quantize_e(n, nc.scalar.copy, part(e_raw, n)))
 
         def product(n, bank, ts, w_first, w_last):
             first, width = PIECES[n]
@@ -157,7 +158,8 @@ def tile_picked_zcft_add_po_kernel(
             cols = slice(first, first + width)
             per_bank = BANK // width
             groups = [range(t0, t0 + per_bank) for t0 in range(0, PACK, per_bank)]
-            g_banks = [psum.tile([P, per_bank, width], F32, name="g%d_%d" % (n, b)) for b in range(len(groups))]
+            g_tags = ["g0", "g1"] if n == 0 else ["g%d" % (n - 1)]
+            g_banks = [psum.tile([P, per_bank, width], F32, name="g%d_%s" % (n, tag), tag=tag) for tag in g_tags]
             h_banks = [psum.tile([P, per_bank, width], F32, name="h%d_%d" % (n, b)) for b in range(len(groups))]
             res = sbuf("res%d" % n, [P, PACK, width], F32)
             res_bf = sbuf("res_bf%d" % n, [P, width, PACK], BF16)
@@ -176,8 +178,10 @@ def tile_picked_zcft_add_po_kernel(
                 rows = slice(ts.start, ts.stop)
                 nc.vector.tensor_tensor(out=res[:, rows, :], in0=bank[:], in1=res[:, rows, :], op=ADD)
             nc.sync.dma_start(out=out_rows[:, :, cols], in_=res[:])
-            last = n == len(PIECES) - 1
-            interleave(nc.vector.tensor_copy if last else nc.scalar.copy, res_bf[:], res[:])
+            split = width // 2 if n == len(PIECES) - 1 else 0
+            if split:
+                interleave(nc.vector.tensor_copy, res_bf[:, :split, :], res[:, :, :split])
+            interleave(nc.scalar.copy, res_bf[:, split:, :], res[:, :, split:])
             nc.vector.quantize_mx(
                 out=res_codes[:].bitcast(FP8X4), scales=out_plane[:, cols], in_=res_bf[:].rearrange("p j t -> p (j t)")
             )

@@ -17,11 +17,14 @@ ADD = mybir.AluOpType.add
 MULT = mybir.AluOpType.mult
 
 P = 128
+QUADRANT = 32
 PACK = 4
 BANK = 512
-PIECES = ((0, 256), (256, 128), (384, 128))
-EARLY = 384
 W1, W2, W3, W4 = range(4)
+
+PIECES = ((0, 256), (256, 128), (384, 128))
+E_EARLY = PIECES[-1][0]
+DEC_EARLY = PIECES[0][1]
 
 
 def interleave(copy, dst, src):
@@ -47,8 +50,11 @@ def tile_picked_zcft_add_po_kernel(
         keep = ctx.enter_context(tc.tile_pool(name="keep", bufs=1))
         psum = ctx.enter_context(tc.psum_pool(name="psum", bufs=1))
 
-        def sbuf(name, shape, dtype, tag=None):
-            return keep.tile(shape, dtype, name=name, tag=tag or name, align_bytes=64)
+        def sbuf(name, shape, dtype, reuse=None):
+            return keep.tile(shape, dtype, name=name, tag=reuse or name, align_bytes=64)
+
+        def live_rows(tile, q):
+            return tile[QUADRANT * q : QUADRANT * q + 4, :].bitcast(I32)
 
         offsets = keep.tile([P, S // 16], U16, name="offsets")
         ws_raw = sbuf("ws_raw", [P, 4 * N], U8)
@@ -59,10 +65,11 @@ def tile_picked_zcft_add_po_kernel(
         x_codes = sbuf("x_codes", [P, S], U32)
         x_plane = sbuf("x_plane", [P, S], U8)
         out_plane = sbuf("out_plane", [P, S], U8)
+        res_codes = sbuf("res_codes", [P, S], U32)
 
         nc.gpsimd.memset(xs_table[:].bitcast(I32), 0)
-        nc.vector.memset(ws_raw[32:64, :].bitcast(I32), 0)
-        nc.vector.memset(ws_raw[64:P, :].bitcast(I32), 0)
+        nc.vector.memset(ws_raw[QUADRANT : 2 * QUADRANT, :].bitcast(I32), 0)
+        nc.vector.memset(ws_raw[2 * QUADRANT : P, :].bitcast(I32), 0)
 
         def load_words(w, queue, raw):
             queue.dma_start(out=raw.bitcast(I32), in_=w_words[w][0].bitcast(I32))
@@ -75,9 +82,7 @@ def tile_picked_zcft_add_po_kernel(
             )
 
         def load_x_scales(q):
-            nc.sync.dma_start(
-                out=xs_table[32 * q : 32 * q + 4, :].bitcast(I32), in_=x_scales[0, 4 * q : 4 * q + 4, :].bitcast(I32)
-            )
+            nc.sync.dma_start(out=live_rows(xs_table, q), in_=x_scales[0, 4 * q : 4 * q + 4, :].bitcast(I32))
 
         def load_rows(rows, cols, raw):
             nc.sync.dma_start(out=raw, in_=rows[:, :, cols])
@@ -92,10 +97,16 @@ def tile_picked_zcft_add_po_kernel(
             nc.vector.quantize_mx(out=codes[:].bitcast(FP8X4), scales=plane[:], in_=grouped[:].rearrange("p j t -> p (j t)"))
             return codes[:], plane[:]
 
-        early, late = slice(0, EARLY), slice(EARLY, S)
+        def part(tiles, early, n):
+            first, width = PIECES[n]
+            if first < early:
+                return tiles[0][:, :, first : first + width]
+            return tiles[1][:, :, first - early : first - early + width]
+
         for w in range(4):
             nc.sync.dma_start(
-                out=ws_raw[0:32, N * w : N * (w + 1)].bitcast(I32), in_=w_scales[w][0].bitcast(I32).partition_broadcast(2)
+                out=ws_raw[0:QUADRANT, N * w : N * (w + 1)].bitcast(I32),
+                in_=w_scales[w][0].bitcast(I32).partition_broadcast(2),
             )
         nc.sync.dma_start(offsets[:], offs)
         ww_raw = {W2: load_words(W2, nc.gpsimd, sbuf("w2_raw", [P, 2 * N], U8)[:])}
@@ -105,44 +116,36 @@ def tile_picked_zcft_add_po_kernel(
         load_x_scales(2)
         load_x_scales(3)
         ww_raw[W1] = load_words(W1, nc.sync, sbuf("w1_raw", [P, 2 * N], U8)[:])
-        e_raw = [load_rows(e_rows, early, sbuf("e_early", [P, PACK, EARLY], F32)[:])]
+        e_raw = [load_rows(e_rows, slice(0, E_EARLY), sbuf("e_early", [P, PACK, E_EARLY], F32)[:])]
+
         nc.vector.tensor_copy(
             out=w_plane[:].rearrange("p (w t b i) -> p w b t i", w=4, t=PACK, i=16),
             in_=ws_raw[:].rearrange("p (w b i t) -> p w b t i", w=4, t=PACK, i=16),
         )
         for q in range(1, 4):
-            nc.sync.dma_start(
-                out=w_plane[32 * q : 32 * q + 4, :].bitcast(I32), in_=w_plane[4 * q : 4 * q + 4, :].bitcast(I32)
-            )
-        dec_sb = [load_rows(dec_rows, early, sbuf("dec_early", [P, PACK, EARLY], F32, "ws_raw")[:])]
+            nc.sync.dma_start(out=live_rows(w_plane, q), in_=w_plane[4 * q : 4 * q + 4, :].bitcast(I32))
+
+        h_raw = sbuf("h_raw", [P, 4 * N], U8, "ws_raw")
+        ww_raw[W4] = load_words(W4, nc.sync, h_raw[:, : 2 * N])
+        ww_raw[W3] = load_words(W3, nc.sync, h_raw[:, 2 * N :])
         nc.vector.tensor_copy(x_codes[:], xw_table[:].indirect(offsets[:]))
-        shift_raw = sbuf("shift_raw", [P, 4 * N], U8, "xw_table")
-        ww_raw[W4] = load_words(W4, nc.sync, shift_raw[:, : 2 * N])
-        ww_raw[W3] = load_words(W3, nc.sync, shift_raw[:, 2 * N :])
+        dec_sb = [load_rows(dec_rows, slice(0, DEC_EARLY), sbuf("dec_early", [P, PACK, DEC_EARLY], F32, "xw_table")[:])]
         nc.vector.tensor_copy(x_plane[:], xs_table[:].indirect(offsets[:]))
-        late_rows = sbuf("late_rows", [P, 2, PACK, S - EARLY], F32, "xs_table")
-        e_raw.append(load_rows(e_rows, late, late_rows[:, 0]))
-        dec_sb.append(load_rows(dec_rows, late, late_rows[:, 1]))
+        e_late, dec_late = PACK * (S - E_EARLY), PACK * (S - DEC_EARLY)
+        late_rows = sbuf("late_rows", [P, e_late + dec_late], F32, "xs_table")
+        e_raw.append(load_rows(e_rows, slice(E_EARLY, S), late_rows[:, :e_late].rearrange("p (t j) -> p t j", t=PACK)))
+        dec_sb.append(load_rows(dec_rows, slice(DEC_EARLY, S), late_rows[:, e_late:].rearrange("p (t j) -> p t j", t=PACK)))
 
-        def part(tiles, n):
-            first, width = PIECES[n]
-            if first < EARLY:
-                return tiles[0][:, :, first : first + width]
-            return tiles[1][:, :, first - EARLY : first - EARLY + width]
-
-        e_mx = [quantize_e(0, nc.vector.tensor_copy, part(e_raw, 0))]
+        e_mx = [quantize_e(0, nc.vector.tensor_copy, part(e_raw, E_EARLY, 0))]
         for n, pair in ((1, (W2, W1)), (2, (W4, W3))):
             for w in pair:
                 deal_words(w, ww_raw[w])
-            e_mx.append(quantize_e(n, nc.scalar.copy, part(e_raw, n)))
+            e_mx.append(quantize_e(n, nc.scalar.copy, part(e_raw, E_EARLY, n)))
 
-        def product(n, bank, ts, w_first, w_last):
+        def product(n, bank, ts, w_x, w_e):
             first, width = PIECES[n]
-            for w in (w_first, w_last):
-                if w in (W1, W3):
-                    codes, plane = e_mx[n]
-                else:
-                    codes, plane = x_codes[:, first : first + width], x_plane[:, first : first + width]
+            x_mx = (x_codes[:, first : first + width], x_plane[:, first : first + width])
+            for w, (codes, plane) in ((w_x, x_mx), (w_e, e_mx[n])):
                 for i, t in enumerate(ts):
                     nc.tensor.matmul_mx(
                         out=bank[:, i, :],
@@ -150,8 +153,8 @@ def tile_picked_zcft_add_po_kernel(
                         lhsT_scale=w_plane[:, N * w + P * t : N * w + P * (t + 1)],
                         rhs=codes.bitcast(FP8X4),
                         rhs_scale=plane,
-                        start=(w == w_first and t == ts[0]),
-                        stop=(w == w_last and t == ts[-1]),
+                        start=(w == w_x and t == ts[0]),
+                        stop=(w == w_e and t == ts[-1]),
                     )
 
         for n, (first, width) in enumerate(PIECES):
@@ -163,8 +166,7 @@ def tile_picked_zcft_add_po_kernel(
             h_banks = [psum.tile([P, per_bank, width], F32, name="h%d_%d" % (n, b)) for b in range(len(groups))]
             res = sbuf("res%d" % n, [P, PACK, width], F32)
             res_bf = sbuf("res_bf%d" % n, [P, width, PACK], BF16)
-            res_codes = sbuf("res_codes%d" % n, [P, width], U32)
-            dec_part = part(dec_sb, n)
+            dec_part = part(dec_sb, DEC_EARLY, n)
             for ts, bank in zip(groups, g_banks):
                 product(n, bank, ts, W2, W1)
             for ts, bank in zip(groups, h_banks):
@@ -183,12 +185,12 @@ def tile_picked_zcft_add_po_kernel(
                 interleave(nc.vector.tensor_copy, res_bf[:, :split, :], res[:, :, :split])
             interleave(nc.scalar.copy, res_bf[:, split:, :], res[:, :, split:])
             nc.vector.quantize_mx(
-                out=res_codes[:].bitcast(FP8X4), scales=out_plane[:, cols], in_=res_bf[:].rearrange("p j t -> p (j t)")
+                out=res_codes[:, cols].bitcast(FP8X4), scales=out_plane[:, cols], in_=res_bf[:].rearrange("p j t -> p (j t)")
             )
-            nc.sync.dma_start(out=out_words[:, cols], in_=res_codes[:].bitcast(I32))
+            if n >= len(PIECES) - 2:
+                done = cols if split else slice(0, first + width)
+                nc.sync.dma_start(out=out_words[:, done], in_=res_codes[:, done].bitcast(I32))
 
         for q in range(4):
             queue = nc.scalar if q % 2 else nc.sync
-            queue.dma_start(
-                out=out_2[0, 4 * q : 4 * q + 4, :].bitcast(I32), in_=out_plane[32 * q : 32 * q + 4, :].bitcast(I32)
-            )
+            queue.dma_start(out=out_2[0, 4 * q : 4 * q + 4, :].bitcast(I32), in_=live_rows(out_plane, q))

from contextlib import ExitStack

import concourse.mybir as mybir

K, T, S, N = 512, 1024, 512, 512
FLOPS = 4 * 2 * K * N * S

F32 = mybir.dt.float32
BF16 = mybir.dt.bfloat16
I32 = mybir.dt.int32
U32 = mybir.dt.uint32
U16 = mybir.dt.uint16
U8 = mybir.dt.uint8
FP8X4 = mybir.dt.float8_e4m3fn_x4
FP4X4 = mybir.dt.float4_e2m1fn_x4
ADD = mybir.AluOpType.add
MULT = mybir.AluOpType.mult

P = 128
QUADRANT = 32
PACK = 4
BANK = 512
W1, W2, W3, W4 = range(4)

PIECES = ((0, 256), (256, 128), (384, 128))
E_EARLY = PIECES[-1][0]
DEC_EARLY = PIECES[0][1]


def interleave(copy, dst, src):
    copy(
        out=dst.rearrange("p (c i) t -> p c t i", i=4),
        in_=src.rearrange("p t (c i) -> p c t i", i=4),
    )


def tile_picked_zcft_add_po_kernel(
    tc, x_words, x_scales, eT, w1_words, w1_scales, w2_words, w2_scales, w3_words, w3_scales,
    w4_words, w4_scales, dec, offs, out_0, out_1, out_2,
):
    nc = tc.nc
    w_words = (w1_words, w2_words, w3_words, w4_words)
    w_scales = (w1_scales, w2_scales, w3_scales, w4_scales)
    e_rows = eT.rearrange("(p t) j -> p t j", t=PACK)
    dec_rows = dec.rearrange("(p t) j -> p t j", t=PACK)
    out_rows = out_0.rearrange("(p t) j -> p t j", t=PACK)
    out_words = out_1[0].rearrange("p j t -> p (j t)").bitcast(I32)

    with ExitStack() as ctx:
        keep = ctx.enter_context(tc.tile_pool(name="keep", bufs=1))
        psum = ctx.enter_context(tc.psum_pool(name="psum", bufs=1))

        def sbuf(name, shape, dtype, reuse=None):
            return keep.tile(shape, dtype, name=name, tag=reuse or name, align_bytes=64)

        def live_rows(tile, q):
            return tile[QUADRANT * q : QUADRANT * q + 4, :].bitcast(I32)

        offsets = keep.tile([P, S // 16], U16, name="offsets")
        ws_raw = sbuf("ws_raw", [P, 4 * N], U8)
        w_plane = sbuf("w_plane", [P, 4 * N], U8)
        ww_dealt = [sbuf("ww_dealt%d" % w, [P, 2 * N], U8) for w in range(4)]
        xw_table = sbuf("xw_table", [P, T], U32)
        xs_table = sbuf("xs_table", [P, T], U8)
        x_codes = sbuf("x_codes", [P, S], U32)
        x_plane = sbuf("x_plane", [P, S], U8)
        out_plane = sbuf("out_plane", [P, S], U8)
        res_codes = sbuf("res_codes", [P, S], U32)

        nc.gpsimd.memset(xs_table[:].bitcast(I32), 0)
        nc.vector.memset(ws_raw[QUADRANT : 2 * QUADRANT, :].bitcast(I32), 0)
        nc.vector.memset(ws_raw[2 * QUADRANT : P, :].bitcast(I32), 0)

        def load_words(w, queue, raw):
            queue.dma_start(out=raw.bitcast(I32), in_=w_words[w][0].bitcast(I32))
            return raw

        def deal_words(w, raw):
            nc.scalar.copy(
                out=ww_dealt[w][:].bitcast(U16).rearrange("p (t b i) -> p b t i", t=PACK, i=8),
                in_=raw.bitcast(U16).rearrange("p (b i t) -> p b t i", t=PACK, i=8),
            )

        def load_x_scales(q):
            nc.sync.dma_start(out=live_rows(xs_table, q), in_=x_scales[0, 4 * q : 4 * q + 4, :].bitcast(I32))

        def load_rows(rows, cols, raw):
            nc.sync.dma_start(out=raw, in_=rows[:, :, cols])
            return raw

        def quantize_e(n, copy, raw):
            width = PIECES[n][1]
            grouped = sbuf("e_bf%d" % n, [P, width, PACK], BF16)
            codes = sbuf("e_codes%d" % n, [P, width], U32)
            plane = sbuf("e_plane%d" % n, [P, width], U8)
            interleave(copy, grouped[:], raw)
            nc.vector.quantize_mx(out=codes[:].bitcast(FP8X4), scales=plane[:], in_=grouped[:].rearrange("p j t -> p (j t)"))
            return codes[:], plane[:]

        def part(tiles, early, n):
            first, width = PIECES[n]
            if first < early:
                return tiles[0][:, :, first : first + width]
            return tiles[1][:, :, first - early : first - early + width]

        for w in range(4):
            nc.sync.dma_start(
                out=ws_raw[0:QUADRANT, N * w : N * (w + 1)].bitcast(I32),
                in_=w_scales[w][0].bitcast(I32).partition_broadcast(2),
            )
        nc.sync.dma_start(offsets[:], offs)
        ww_raw = {W2: load_words(W2, nc.gpsimd, sbuf("w2_raw", [P, 2 * N], U8)[:])}
        load_x_scales(0)
        load_x_scales(1)
        nc.sync.dma_start(out=xw_table[:].bitcast(I32), in_=x_words[0].rearrange("p n t -> p (n t)").bitcast(I32))
        load_x_scales(2)
        load_x_scales(3)
        ww_raw[W1] = load_words(W1, nc.sync, sbuf("w1_raw", [P, 2 * N], U8)[:])
        e_raw = [load_rows(e_rows, slice(0, E_EARLY), sbuf("e_early", [P, PACK, E_EARLY], F32)[:])]

        nc.vector.tensor_copy(
            out=w_plane[:].rearrange("p (w t b i) -> p w b t i", w=4, t=PACK, i=16),
            in_=ws_raw[:].rearrange("p (w b i t) -> p w b t i", w=4, t=PACK, i=16),
        )
        for q in range(1, 4):
            nc.sync.dma_start(out=live_rows(w_plane, q), in_=w_plane[4 * q : 4 * q + 4, :].bitcast(I32))

        h_raw = sbuf("h_raw", [P, 4 * N], U8, "ws_raw")
        ww_raw[W4] = load_words(W4, nc.sync, h_raw[:, : 2 * N])
        ww_raw[W3] = load_words(W3, nc.sync, h_raw[:, 2 * N :])
        nc.vector.tensor_copy(x_codes[:], xw_table[:].indirect(offsets[:]))
        dec_sb = [load_rows(dec_rows, slice(0, DEC_EARLY), sbuf("dec_early", [P, PACK, DEC_EARLY], F32, "xw_table")[:])]
        nc.vector.tensor_copy(x_plane[:], xs_table[:].indirect(offsets[:]))
        e_late, dec_late = PACK * (S - E_EARLY), PACK * (S - DEC_EARLY)
        late_rows = sbuf("late_rows", [P, e_late + dec_late], F32, "xs_table")
        e_raw.append(load_rows(e_rows, slice(E_EARLY, S), late_rows[:, :e_late].rearrange("p (t j) -> p t j", t=PACK)))
        dec_sb.append(load_rows(dec_rows, slice(DEC_EARLY, S), late_rows[:, e_late:].rearrange("p (t j) -> p t j", t=PACK)))

        e_mx = [quantize_e(0, nc.vector.tensor_copy, part(e_raw, E_EARLY, 0))]
        for n, pair in ((1, (W2, W1)), (2, (W4, W3))):
            for w in pair:
                deal_words(w, ww_raw[w])
            e_mx.append(quantize_e(n, nc.scalar.copy, part(e_raw, E_EARLY, n)))

        def product(n, bank, ts, w_x, w_e):
            first, width = PIECES[n]
            x_mx = (x_codes[:, first : first + width], x_plane[:, first : first + width])
            for w, (codes, plane) in ((w_x, x_mx), (w_e, e_mx[n])):
                for i, t in enumerate(ts):
                    nc.tensor.matmul_mx(
                        out=bank[:, i, :],
                        lhsT=ww_dealt[w][:, 2 * P * t : 2 * P * (t + 1)].bitcast(FP4X4),
                        lhsT_scale=w_plane[:, N * w + P * t : N * w + P * (t + 1)],
                        rhs=codes.bitcast(FP8X4),
                        rhs_scale=plane,
                        start=(w == w_x and t == ts[0]),
                        stop=(w == w_e and t == ts[-1]),
                    )

        for n, (first, width) in enumerate(PIECES):
            cols = slice(first, first + width)
            per_bank = BANK // width
            groups = [range(t0, t0 + per_bank) for t0 in range(0, PACK, per_bank)]
            g_tags = ["g0", "g1"] if n == 0 else ["g%d" % (n - 1)]
            g_banks = [psum.tile([P, per_bank, width], F32, name="g%d_%s" % (n, tag), tag=tag) for tag in g_tags]
            h_banks = [psum.tile([P, per_bank, width], F32, name="h%d_%d" % (n, b)) for b in range(len(groups))]
            res = sbuf("res%d" % n, [P, PACK, width], F32)
            res_bf = sbuf("res_bf%d" % n, [P, width, PACK], BF16)
            dec_part = part(dec_sb, DEC_EARLY, n)
            for ts, bank in zip(groups, g_banks):
                product(n, bank, ts, W2, W1)
            for ts, bank in zip(groups, h_banks):
                product(n, bank, ts, W4, W3)
            for ts, bank in zip(groups, g_banks):
                rows = slice(ts.start, ts.stop)
                nc.vector.scalar_tensor_tensor(
                    out=res[:, rows, :], in0=bank[:], scalar=1.0, in1=dec_part[:, rows, :], op0=ADD, op1=MULT
                )
            for ts, bank in zip(groups, h_banks):
                rows = slice(ts.start, ts.stop)
                nc.vector.tensor_tensor(out=res[:, rows, :], in0=bank[:], in1=res[:, rows, :], op=ADD)
            nc.sync.dma_start(out=out_rows[:, :, cols], in_=res[:])
            split = width // 2 if n == len(PIECES) - 1 else 0
            if split:
                interleave(nc.vector.tensor_copy, res_bf[:, :split, :], res[:, :, :split])
            interleave(nc.scalar.copy, res_bf[:, split:, :], res[:, :, split:])
            nc.vector.quantize_mx(
                out=res_codes[:, cols].bitcast(FP8X4), scales=out_plane[:, cols], in_=res_bf[:].rearrange("p j t -> p (j t)")
            )
            if n >= len(PIECES) - 2:
                done = cols if split else slice(0, first + width)
                nc.sync.dma_start(out=out_words[:, done], in_=res_codes[:, done].bitcast(I32))

        for q in range(4):
            queue = nc.scalar if q % 2 else nc.sync
            queue.dma_start(out=out_2[0, 4 * q : 4 * q + 4, :].bitcast(I32), in_=live_rows(out_plane, q))
